import numpy as np
import ml_dtypes


def mxq(x, axis, fmt="e4m3"):
    dtype, down = {"e4m3": (ml_dtypes.float8_e4m3fn, 7), "e5m2": (ml_dtypes.float8_e5m2, 14)}[fmt]
    v = np.moveaxis(np.asarray(x, np.float32).astype(ml_dtypes.bfloat16).astype(np.float64), axis, -1)
    blocks = v.reshape(v.shape[:-1] + (-1, 32))
    amax = np.abs(blocks).max(-1, keepdims=True)
    byte = np.maximum(np.where(amax > 0, np.frexp(amax)[1] - 1 + 127, 0) - down, 1)
    scale = np.exp2(byte - 127.0)
    codes = (blocks / scale).astype(np.float32).astype(dtype).astype(np.float64)
    return np.moveaxis((codes * scale).reshape(v.shape), -1, axis)


WIDE = False


def mx_kscale(k):
    if not WIDE:
        return np.ones(k)
    levels = np.array([10, -10, 5, -5, 0])
    if k % 512:
        return np.exp2(np.random.permutation(np.resize(levels, k // 32))).repeat(32)
    a = np.empty((k // 512, 16))
    for p in range(k // 512):
        a[p, :8] = np.random.permutation(np.resize(levels, 8))
        for g in range(8):
            far = levels[np.abs(levels - a[p, g]) >= 10]
            a[p, g + 8] = far[np.random.randint(len(far))]
    return np.exp2(a.ravel()).repeat(32)


def f64(x):
    return np.asarray(x).astype(np.float64)


def striped(idx):
    return np.tile(idx.reshape(-1, 16).T, (8, 1)).astype(np.uint16)


def unstriped(offs):
    return offs[:16].T.reshape(-1).astype(np.int64)


E2M1 = np.array([0.0, 0.5, 1.0, 1.5, 2.0, 3.0, 4.0, 6.0, -0.0, -0.5, -1.0, -1.5, -2.0, -3.0, -4.0, -6.0])


def pack_weight(w, fmt):
    k, n = w.shape
    w = f64(np.asarray(w, np.float32).astype(ml_dtypes.bfloat16)).reshape(k // 32, 32, n)
    amax = np.abs(w).max(1)
    if fmt == "e4m3":
        byte = np.frexp(amax)[1] - 1 + 127 - 7
    else:
        mant, ex = np.frexp(amax / 6.0)
        byte = np.where(mant > 0.5, ex, ex - 1) + 127
    byte = np.clip(np.where(amax > 0, byte, 1), 1, 254)
    scaled = (w * np.exp2(127.0 - byte)[:, None, :]).reshape(k, n).astype(np.float32)
    by_word = np.ascontiguousarray(scaled.reshape(k // 512, 128, 4, n).transpose(0, 1, 3, 2))
    if fmt == "e4m3":
        words = by_word.astype(ml_dtypes.float8_e4m3fn).view(np.uint8)
    else:
        c = by_word.astype(ml_dtypes.float4_e2m1fn).view(np.uint8) & 0xF
        words = (c[..., 0::2] | (c[..., 1::2] << 4)).reshape(k // 512, 128, 2 * n)
    return np.ascontiguousarray(words), np.ascontiguousarray(byte.astype(np.uint8).reshape(k // 512, 16, n))


def unpack_weight(words, scales, fmt):
    g, _, n = scales.shape
    words = np.ascontiguousarray(words).reshape(g, 128, n, -1)
    if fmt == "e4m3":
        vals = words.view(ml_dtypes.float8_e4m3fn).astype(np.float64)
    else:
        nib = np.empty((g, 128, n, 4), np.uint8)
        nib[..., 0::2] = words & 0xF
        nib[..., 1::2] = words >> 4
        vals = E2M1[nib]
    vals = vals * np.repeat(np.exp2(scales.astype(np.float64) - 127.0), 8, axis=1)[..., None]
    return vals.transpose(0, 1, 3, 2).reshape(g * 512, n)


def gelu(v):
    return 0.5 * v * (1.0 + np.tanh(np.sqrt(2.0 / np.pi) * (v + 0.044715 * v**3)))


def striped8(idx):
    return np.concatenate([v.reshape(-1, 16).T for v in idx]).astype(np.uint16)


def unstriped8(offs):
    return np.stack([offs[16 * g:16 * g + 16].T.reshape(-1) for g in range(8)]).astype(np.int64)


def heads(h, wgt, idx8):
    r = np.arange(h.shape[0])
    return wgt[r // 4 % 128] * h[r[:, None], idx8[r % 512 // 64]]


def put_heads(h, wgs, idx8, t2):
    r = np.arange(h.shape[0])
    page = np.zeros((h.shape[0], t2))
    page[r[:, None], idx8[r % 512 // 64]] = wgs[r // 4 % 128] * h
    return page


K, T, S, H, P, T2, N = 1536, 4096, 1024, 512, 512, 1024, 1024

def setup_inputs():
    n = np.random.standard_normal
    s = mx_kscale(K)[:, None]
    u = mx_kscale(H)[:, None]
    d = {}
    d["tab_words"], d["tab_scales"] = pack_weight(n((K, T)) * s, "e4m3")
    d["offs"] = striped(np.random.permutation(T)[:S])
    d["w1_words"], d["w1_scales"] = pack_weight(1.5 * n((K, H)) / K ** 0.5 / s, "e2m1")
    d["w2"] = (1.2 * n((K, H)) / K ** 0.5 / s).astype(np.float32)
    d["gain"] = (np.exp(0.3 * n(H)) * u[:, 0]).astype(np.float32)
    d["offs2"] = striped8(np.stack([np.random.permutation(S)[:P] for _ in range(8)]))
    d["wgt"] = np.repeat(np.random.uniform(0.5, 2.0, (8, P)), 16, axis=0).astype(np.float32)
    d["taste"] = np.exp(0.3 * n(H)).astype(np.float32)
    d["season"] = (0.7 * n((H, P)) * u).astype(np.float32)
    d["w3_words"], d["w3_scales"] = pack_weight(n((H, N)) / H ** 0.5 / u, "e4m3")
    d["offs3"] = striped8(np.stack([np.random.permutation(T2)[:P] for _ in range(8)]))
    d["wgo"] = np.repeat(np.random.uniform(0.5, 2.0, (8, P)), 16, axis=0).astype(np.float32)
    return d

def reference(tab_words, tab_scales, offs, w1_words, w1_scales, w2, gain, offs2, wgt, taste, season, w3_words, w3_scales, offs3, wgo):
    v = unpack_weight(tab_words, tab_scales, "e4m3")[:, unstriped(offs)]
    a = unpack_weight(w1_words, w1_scales, "e2m1").T @ v
    b = mxq(f64(w2), 0, "e4m3").T @ v
    vigour = 0.5 * a * (1.0 + np.tanh(0.7978845608 * (a + 0.044715 * a ** 3)))
    h = np.minimum(vigour, b) * f64(gain)[:, None]
    x = heads(h, f64(wgt), unstriped8(offs2))
    z = x * f64(taste)[:, None] + f64(season)
    e = unpack_weight(w3_words, w3_scales, "e4m3").T @ mxq(z, 0, "e4m3")
    y = 1.0 / (1.0 + e * e)
    return put_heads(y, f64(wgo), unstriped8(offs3), T2)

@@ -1,0 +1,230 @@
+from contextlib import ExitStack
+
+import concourse.mybir as mybir
+
+F32 = mybir.dt.float32
+BF16 = mybir.dt.bfloat16
+I32 = mybir.dt.int32
+U32 = mybir.dt.uint32
+U16 = mybir.dt.uint16
+U8 = mybir.dt.uint8
+FP8X4 = mybir.dt.float8_e4m3fn_x4
+FP4X4 = mybir.dt.float4_e2m1fn_x4
+ACT = mybir.ActivationFunctionType
+ALU = mybir.AluOpType
+
+K, T, S, H, M, T2, N = 1536, 4096, 1024, 512, 512, 1024, 1024
+FLOPS = 2 * (2 * K * H * S + H * N * M)
+
+P = 128
+PACK = 4
+PASSES = K // (P * PACK)
+BANK = 512
+PAGES = 4
+SLOT = 4 * T
+SPLIT_TILES = 2
+
+
+def tile_list_bonsai_restraint_scores_kernel(
+    tc, tab_words, tab_scales, offs, w1_words, w1_scales, w2, gain, offs2, wgt, taste, season,
+    w3_words, w3_scales, offs3, wgo, out,
+):
+    nc = tc.nc
+    with ExitStack() as ctx:
+        keep = ctx.enter_context(tc.tile_pool(name="keep", bufs=1))
+        arena = ctx.enter_context(tc.tile_pool(name="arena", bufs=1))
+        ring = ctx.enter_context(tc.tile_pool(name="ring", bufs=4))
+        psum = ctx.enter_context(tc.psum_pool(name="psum", bufs=1))
+
+        def held(name, shape, dtype):
+            return keep.tile(shape, dtype, name=name, align_bytes=64)
+
+        def bank(index):
+            return psum.tile([P, BANK], F32, name="bank%d" % index)
+
+        def staged(name, shape, dtype, offset):
+            return arena.tile(shape, dtype, name=name, align_bytes=64, offset=offset)
+
+        idx = keep.tile([P, S // 16], U16, name="idx")
+        idx2 = keep.tile([P, M // 16], U16, name="idx2")
+        idx3 = keep.tile([P, M // 16], U16, name="idx3")
+        tab_sc = held("tab_sc", [P, T], U8)
+        w1_sc_raw = held("w1_sc_raw", [P, PASSES, H], U8)
+        v_sc = [held("v_sc%d" % a, [P, S], U8) for a in range(PASSES)]
+
+        nc.vector.memset(tab_sc[:].bitcast(I32), 0)
+        nc.vector.memset(w1_sc_raw[:].rearrange("p a c -> p (a c)").bitcast(I32), 0)
+        for plane in v_sc:
+            nc.vector.memset(plane[:].bitcast(I32), 0)
+
+        def load_table(a):
+            words = staged("tab%d" % a, [P, T], U32, a * SLOT)
+            nc.sync.dma_start(out=words[:].bitcast(I32),
+                              in_=tab_words[a].rearrange("p t i -> p (t i)").bitcast(I32))
+            return words
+
+        gain_sb = held("gain_sb", [P, PACK], F32)
+        taste_sb = held("taste_sb", [P, PACK], F32)
+        nc.gpsimd.dma_start(out=gain_sb[:], in_=gain.rearrange("(p i) -> p i", i=PACK))
+        nc.gpsimd.dma_start(out=taste_sb[:], in_=taste.rearrange("(p i) -> p i", i=PACK))
+        nc.sync.dma_start(idx[:], offs)
+        nc.sync.dma_start(idx2[:], offs2)
+        nc.sync.dma_start(idx3[:], offs3)
+        w1_raw = staged("w1_raw", [P, PASSES, 2 * H], U8, 2 * SLOT - PASSES * H)
+        nc.sync.dma_start(out=w1_raw[:].bitcast(I32), in_=w1_words.rearrange("a p c -> p a c").bitcast(I32))
+        tab = [load_table(0)]
+        nc.sync.dma_start(out=tab_sc[0:P:4, :].bitcast(I32),
+                          in_=tab_scales[0:2].rearrange("a q t -> (a q) t").bitcast(I32))
+        nc.sync.dma_start(out=tab_sc[2:P:8, :].bitcast(I32), in_=tab_scales[2].bitcast(I32))
+        for q in range(4):
+            nc.scalar.dma_start(out=w1_sc_raw[32 * q:32 * q + 4].bitcast(I32),
+                                in_=w1_scales[:, 4 * q:4 * q + 4, :].rearrange("a r c -> r a c").bitcast(I32))
+
+        w1_q = held("w1_q", [P, PASSES, 2 * H], U8)
+        w1_sc = held("w1_sc", [P, PASSES, H], U8)
+        nc.scalar.copy(out=w1_q[:].bitcast(U16).rearrange("p a (i m) -> p a m i", i=PACK),
+                       in_=w1_raw[:].bitcast(U16).rearrange("p a (m i) -> p a m i", i=PACK))
+        tab.extend([load_table(1), load_table(2)])
+        picked_sc = held("picked_sc", [P, S], U8)
+        nc.vector.tensor_copy(picked_sc[:], tab_sc[:].indirect(idx[:]))
+        nc.vector.tensor_copy(out=w1_sc[:].rearrange("p a (i m) -> p a m i", i=PACK),
+                              in_=w1_sc_raw[:].rearrange("p a (m i) -> p a m i", i=PACK))
+        for a in range(PASSES):
+            queue = nc.scalar if a == 0 else nc.gpsimd
+            for q in range(4):
+                first, step = (64 * a + 16 * q, 4) if a < 2 else (2 + 32 * q, 8)
+                queue.dma_start(out=v_sc[a][32 * q:32 * q + 4, :].bitcast(I32),
+                                in_=picked_sc[first:first + 3 * step + 1:step, :].bitcast(I32))
+        v = {}
+        for a in range(PASSES):
+            for half in range(2):
+                v[a, half] = held("v%d_%d" % (a, half), [P, BANK], U32)
+                nc.vector.tensor_copy(v[a, half][:], tab[a][:].indirect(idx[:, 32 * half:32 * (half + 1)]))
+
+        w2_raw = []
+        for a in range(PASSES):
+            w2_raw.append(staged("w2_raw%d" % a, [P, PACK, H], F32, a * SLOT // 2))
+            nc.sync.dma_start(out=w2_raw[a][:],
+                              in_=w2[512 * a:512 * (a + 1), :].rearrange("(p j) c -> p j c", j=PACK))
+        wgt_sb = staged("wgt_sb", [P, M], F32, 3 * SLOT // 2)
+        nc.sync.dma_start(out=wgt_sb[:], in_=wgt)
+        w3_sc_raw = staged("w3_sc_raw", [P, N], U8, 3 * SLOT - 4 * M - N)
+        nc.vector.memset(w3_sc_raw[:].bitcast(I32), 0)
+        w3_raw = staged("w3_raw", [P, N], U32, 2 * SLOT)
+        nc.sync.dma_start(out=w3_raw[:].bitcast(I32), in_=w3_words[0].rearrange("p c i -> p (c i)").bitcast(I32))
+        season_sb = staged("season_sb", [P, PACK, M], F32, 2 * SLOT + 4 * N)
+        nc.sync.dma_start(out=season_sb[:], in_=season.rearrange("(p i) m -> p i m", i=PACK))
+        wgo_sb = staged("wgo_sb", [P, M], F32, 3 * SLOT - 4 * M)
+        nc.sync.dma_start(out=wgo_sb[:], in_=wgo)
+        for q in range(4):
+            nc.sync.dma_start(out=w3_sc_raw[32 * q:32 * q + 4, :].bitcast(I32),
+                              in_=w3_scales[0, 4 * q:4 * q + 4, :].bitcast(I32))
+
+        groups = [(i, half) for half in range(2) for i in range(PACK)]
+        acc_a = {(i, half): bank(2 * i + half) for i, half in groups}
+        g = {}
+        for a in range(PASSES):
+            for i, half in groups:
+                nc.tensor.matmul_mx(
+                    out=acc_a[i, half][:],
+                    lhsT=w1_q[:, a, 256 * i:256 * (i + 1)].bitcast(FP4X4),
+                    lhsT_scale=w1_sc[:, a, P * i:P * (i + 1)],
+                    rhs=v[a, half][:].bitcast(FP8X4),
+                    rhs_scale=v_sc[a][:, BANK * half:BANK * (half + 1)],
+                    start=(a == 0), stop=(a == PASSES - 1))
+        for i, half in groups:
+            g[i, half] = held("g%d_%d" % (i, half), [P, BANK], F32)
+            nc.scalar.activation(out=g[i, half][:], in_=acc_a[i, half][:], func=ACT.Gelu_apprx_tanh)
+
+        w2_q = {}
+        w2_sc = {}
+        for a in range(PASSES):
+            for pair in range(2):
+                rounded = ring.tile([P, 2 * P * PACK], BF16, name="rounded", align_bytes=64)
+                src = w2_raw[a][:].rearrange("p j (m i) -> p m i j", i=PACK)[:, :, 2 * pair:2 * pair + 2, :]
+                dst = rounded[:].rearrange("p (i m j) -> p m i j", i=2, j=PACK)
+                if a == PASSES - 1 and pair == 1:
+                    nc.scalar.copy(out=dst, in_=src)
+                else:
+                    nc.vector.tensor_copy(out=dst, in_=src)
+                w2_q[a, pair] = held("w2_q%d_%d" % (a, pair), [P, 2 * P], U32)
+                w2_sc[a, pair] = held("w2_sc%d_%d" % (a, pair), [P, 2 * P], U8)
+                nc.vector.quantize_mx(out=w2_q[a, pair][:].bitcast(FP8X4), scales=w2_sc[a, pair][:], in_=rounded[:])
+
+        acc_b = {(i, half): bank(2 * i + half) for i, half in groups}
+        by_row = [(i, half) for i in range(PACK) for half in range(2)]
+        for a in range(PASSES):
+            for i, half in (by_row if a == PASSES - 1 else groups):
+                cols = slice(P * (i % 2), P * (i % 2 + 1))
+                nc.tensor.matmul_mx(
+                    out=acc_b[i, half][:],
+                    lhsT=w2_q[a, i // 2][:, cols].bitcast(FP8X4),
+                    lhsT_scale=w2_sc[a, i // 2][:, cols],
+                    rhs=v[a, half][:].bitcast(FP8X4),
+                    rhs_scale=v_sc[a][:, BANK * half:BANK * (half + 1)],
+                    start=(a == 0), stop=(a == PASSES - 1))
+
+        wt = held("wt", [P, PACK, M], F32)
+        for i in range(PACK):
+            nc.scalar.activation(out=wt[:, i, :], in_=wgt_sb[:], func=ACT.Copy, scale=taste_sb[:, i:i + 1])
+
+        h = [held("h%d" % i, [P, S], F32) for i in range(PACK)]
+        for i, half in by_row:
+            nc.vector.tensor_tensor(out=g[i, half][:], in0=acc_b[i, half][:], in1=g[i, half][:], op=ALU.min)
+            nc.scalar.activation(out=h[i][:, BANK * half:BANK * (half + 1)], in_=g[i, half][:], func=ACT.Copy,
+                                 scale=gain_sb[:, i:i + 1])
+
+        w3_q = held("w3_q", [P, N], U32)
+        nc.scalar.copy(out=w3_q[:].rearrange("p (b i m) -> p b m i", b=2, i=PACK),
+                       in_=w3_raw[:].rearrange("p (b m i) -> p b m i", b=2, i=PACK))
+
+        w3_sc = held("w3_sc", [P, N], U8)
+        nc.vector.tensor_copy(out=w3_sc[:].rearrange("p (b i m) -> p b m i", b=2, i=PACK),
+                              in_=w3_sc_raw[:].rearrange("p (b m i) -> p b m i", b=2, i=PACK))
+
+        HM = M // 2
+        z_q = held("z_q", [P, M], U32)
+        z_sc = held("z_sc", [P, M], U8)
+        for half in range(2):
+            cols = slice(HM * half, HM * (half + 1))
+            x = held("x%d" % half, [P, PACK, HM], F32)
+            for i in range(PACK):
+                nc.vector.tensor_tensor(x[:, i, :], h[i][:].indirect(idx2[:, 16 * half:16 * (half + 1)]),
+                                        wt[:, i, cols], ALU.mult)
+            z = held("z%d" % half, [P, HM * PACK], BF16)
+            nc.vector.tensor_tensor(out=z[:].rearrange("p (c u i) -> p c i u", u=4, i=PACK),
+                                    in0=x[:].rearrange("p i (c u) -> p c i u", u=4),
+                                    in1=season_sb[:, :, cols].rearrange("p i (c u) -> p c i u", u=4), op=ALU.add)
+            nc.vector.quantize_mx(out=z_q[:, cols].bitcast(FP8X4), scales=z_sc[:, cols], in_=z[:])
+
+        pages = [held("page%d" % b, [P, T2], F32) for b in range(PAGES)]
+        for page in pages:
+            nc.vector.memset(page[:], 0.0)
+        out_rows = out.rearrange("(b p i) c -> b i p c", b=2, i=PACK)
+
+        def place(tile_n, first, count, bank_index):
+            cols = slice(first, first + count)
+            acc = bank(bank_index)
+            nc.tensor.matmul_mx(
+                out=acc[:, 0:count],
+                lhsT=w3_q[:, P * tile_n:P * (tile_n + 1)].bitcast(FP8X4),
+                lhsT_scale=w3_sc[:, P * tile_n:P * (tile_n + 1)],
+                rhs=z_q[:, cols].bitcast(FP8X4), rhs_scale=z_sc[:, cols], start=True, stop=True)
+            y = ring.tile([P, M], F32, name="y")
+            nc.scalar.activation(out=y[:, 0:count], in_=acc[:, 0:count], func=ACT.Square)
+            nc.scalar.activation(out=y[:, 0:count], in_=y[:, 0:count], func=ACT.Abs_reciprocal_sqrt, bias=1.0)
+            nc.scalar.activation(out=y[:, 0:count], in_=y[:, 0:count], func=ACT.Square)
+            nc.vector.tensor_tensor(pages[tile_n % PAGES][:].indirect(idx3[:, first // 16:(first + count) // 16]),
+                                    y[:, 0:count], wgo_sb[:, cols], ALU.mult)
+
+        def store(tile_n):
+            nc.sync.dma_start(out=out_rows[tile_n // PACK, tile_n % PACK], in_=pages[tile_n % PAGES][:])
+
+        for tile_n in range(SPLIT_TILES):
+            place(tile_n, 0, HM, tile_n)
+        for tile_n in range(SPLIT_TILES):
+            place(tile_n, HM, HM, SPLIT_TILES + tile_n)
+            store(tile_n)
+        for tile_n in range(SPLIT_TILES, N // P):
+            place(tile_n, 0, M, (SPLIT_TILES + tile_n) % 8)
+            store(tile_n)

@@ -20,8 +20,9 @@ P = 128
 PACK = 4
 PASSES = K // (P * PACK)
 BANK = 512
-PAGES = 4
+PAGES = 3
 SLOT = 4 * T
+SC_AT = 5 * SLOT // 2 + 1024
 SPLIT_TILES = 2
 
 
@@ -48,7 +49,7 @@ def tile_list_bonsai_restraint_scores_kernel(
         idx = keep.tile([P, S // 16], U16, name="idx")
         idx2 = keep.tile([P, M // 16], U16, name="idx2")
         idx3 = keep.tile([P, M // 16], U16, name="idx3")
-        tab_sc = held("tab_sc", [P, T], U8)
+        tab_sc = staged("tab_sc", [P, T], U8, SC_AT)
         w1_sc_raw = held("w1_sc_raw", [P, PASSES, H], U8)
         v_sc = [held("v_sc%d" % a, [P, S], U8) for a in range(PASSES)]
 
@@ -58,21 +59,28 @@ def tile_list_bonsai_restraint_scores_kernel(
             nc.vector.memset(plane[:].bitcast(I32), 0)
 
         def load_table(a):
-            words = staged("tab%d" % a, [P, T], U32, a * SLOT)
+            words = staged("tab%d" % a, [P, T], U32, a % 2 * SLOT)
             nc.sync.dma_start(out=words[:].bitcast(I32),
                               in_=tab_words[a].rearrange("p t i -> p (t i)").bitcast(I32))
             return words
+
+        def load_w2(a, offset):
+            rows = staged("w2_raw%d" % a, [P, PACK, H], F32, offset)
+            nc.sync.dma_start(out=rows[:], in_=w2[512 * a:512 * (a + 1), :].rearrange("(p j) c -> p j c", j=PACK))
+            return rows
 
         gain_sb = held("gain_sb", [P, PACK], F32)
         taste_sb = held("taste_sb", [P, PACK], F32)
         nc.gpsimd.dma_start(out=gain_sb[:], in_=gain.rearrange("(p i) -> p i", i=PACK))
         nc.gpsimd.dma_start(out=taste_sb[:], in_=taste.rearrange("(p i) -> p i", i=PACK))
+        w1_raw = staged("w1_raw", [P, PASSES, 2 * H], U8, SLOT - PASSES * H)
+        nc.sync.dma_start(out=w1_raw[:].bitcast(I32), in_=w1_words.rearrange("a p c -> p a c").bitcast(I32))
         nc.sync.dma_start(idx[:], offs)
+        w2_raw = [load_w2(0, 2 * SLOT)]
         nc.sync.dma_start(idx2[:], offs2)
         nc.sync.dma_start(idx3[:], offs3)
-        w1_raw = staged("w1_raw", [P, PASSES, 2 * H], U8, 2 * SLOT - PASSES * H)
-        nc.sync.dma_start(out=w1_raw[:].bitcast(I32), in_=w1_words.rearrange("a p c -> p a c").bitcast(I32))
-        tab = [load_table(0)]
+        wgt_sb = held("wgt_sb", [P, M], F32)
+        nc.sync.dma_start(out=wgt_sb[:], in_=wgt)
         nc.sync.dma_start(out=tab_sc[0:P:4, :].bitcast(I32),
                           in_=tab_scales[0:2].rearrange("a q t -> (a q) t").bitcast(I32))
         nc.sync.dma_start(out=tab_sc[2:P:8, :].bitcast(I32), in_=tab_scales[2].bitcast(I32))
@@ -81,41 +89,35 @@ def tile_list_bonsai_restraint_scores_kernel(
                                 in_=w1_scales[:, 4 * q:4 * q + 4, :].rearrange("a r c -> r a c").bitcast(I32))
 
         w1_q = held("w1_q", [P, PASSES, 2 * H], U8)
-        w1_sc = held("w1_sc", [P, PASSES, H], U8)
-        nc.scalar.copy(out=w1_q[:].bitcast(U16).rearrange("p a (i m) -> p a m i", i=PACK),
-                       in_=w1_raw[:].bitcast(U16).rearrange("p a (m i) -> p a m i", i=PACK))
-        tab.extend([load_table(1), load_table(2)])
+        nc.vector.tensor_copy(out=w1_q[:].bitcast(U16).rearrange("p a (i m) -> p a m i", i=PACK),
+                              in_=w1_raw[:].bitcast(U16).rearrange("p a (m i) -> p a m i", i=PACK))
+        tab = [load_table(0), load_table(1)]
         picked_sc = held("picked_sc", [P, S], U8)
         nc.vector.tensor_copy(picked_sc[:], tab_sc[:].indirect(idx[:]))
+        w1_sc = staged("w1_sc", [P, PASSES, H], U8, SC_AT + 1024)
         nc.vector.tensor_copy(out=w1_sc[:].rearrange("p a (i m) -> p a m i", i=PACK),
                               in_=w1_sc_raw[:].rearrange("p a (m i) -> p a m i", i=PACK))
         for a in range(PASSES):
-            queue = nc.scalar if a == 0 else nc.gpsimd
             for q in range(4):
                 first, step = (64 * a + 16 * q, 4) if a < 2 else (2 + 32 * q, 8)
+                queue = nc.scalar if a < 2 and q < 3 else nc.gpsimd
                 queue.dma_start(out=v_sc[a][32 * q:32 * q + 4, :].bitcast(I32),
-                                in_=picked_sc[first:first + 3 * step + 1:step, :].bitcast(I32))
+                                    in_=picked_sc[first:first + 3 * step + 1:step, :].bitcast(I32))
         v = {}
         for a in range(PASSES):
             for half in range(2):
                 v[a, half] = held("v%d_%d" % (a, half), [P, BANK], U32)
                 nc.vector.tensor_copy(v[a, half][:], tab[a][:].indirect(idx[:, 32 * half:32 * (half + 1)]))
+            if a == 0:
+                tab.append(load_table(2))
 
-        w2_raw = []
-        for a in range(PASSES):
-            w2_raw.append(staged("w2_raw%d" % a, [P, PACK, H], F32, a * SLOT // 2))
-            nc.sync.dma_start(out=w2_raw[a][:],
-                              in_=w2[512 * a:512 * (a + 1), :].rearrange("(p j) c -> p j c", j=PACK))
-        wgt_sb = staged("wgt_sb", [P, M], F32, 3 * SLOT // 2)
-        nc.sync.dma_start(out=wgt_sb[:], in_=wgt)
-        w3_sc_raw = staged("w3_sc_raw", [P, N], U8, 3 * SLOT - 4 * M - N)
+        w2_raw.extend([load_w2(1, SLOT), load_w2(2, 3 * SLOT // 2)])
+        w3_sc_raw = staged("w3_sc_raw", [P, N], U8, 4 * M)
         nc.vector.memset(w3_sc_raw[:].bitcast(I32), 0)
-        w3_raw = staged("w3_raw", [P, N], U32, 2 * SLOT)
+        w3_raw = staged("w3_raw", [P, N], U32, 4 * M + N)
         nc.sync.dma_start(out=w3_raw[:].bitcast(I32), in_=w3_words[0].rearrange("p c i -> p (c i)").bitcast(I32))
-        season_sb = staged("season_sb", [P, PACK, M], F32, 2 * SLOT + 4 * N)
+        season_sb = staged("season_sb", [P, PACK, M], F32, 4 * M + 5 * N)
         nc.sync.dma_start(out=season_sb[:], in_=season.rearrange("(p i) m -> p i m", i=PACK))
-        wgo_sb = staged("wgo_sb", [P, M], F32, 3 * SLOT - 4 * M)
-        nc.sync.dma_start(out=wgo_sb[:], in_=wgo)
         for q in range(4):
             nc.sync.dma_start(out=w3_sc_raw[32 * q:32 * q + 4, :].bitcast(I32),
                               in_=w3_scales[0, 4 * q:4 * q + 4, :].bitcast(I32))
@@ -140,7 +142,7 @@ def tile_list_bonsai_restraint_scores_kernel(
         w2_sc = {}
         for a in range(PASSES):
             for pair in range(2):
-                rounded = ring.tile([P, 2 * P * PACK], BF16, name="rounded", align_bytes=64)
+                rounded = staged("rounded%d" % pair, [P, 2 * P * PACK], BF16, SC_AT - 1024 + pair * 3584)
                 src = w2_raw[a][:].rearrange("p j (m i) -> p m i j", i=PACK)[:, :, 2 * pair:2 * pair + 2, :]
                 dst = rounded[:].rearrange("p (i m j) -> p m i j", i=2, j=PACK)
                 if a == PASSES - 1 and pair == 1:
@@ -151,10 +153,14 @@ def tile_list_bonsai_restraint_scores_kernel(
                 w2_sc[a, pair] = held("w2_sc%d_%d" % (a, pair), [P, 2 * P], U8)
                 nc.vector.quantize_mx(out=w2_q[a, pair][:].bitcast(FP8X4), scales=w2_sc[a, pair][:], in_=rounded[:])
 
+        wgo_sb = staged("wgo_sb", [P, M], F32, SLOT)
+        nc.sync.dma_start(out=wgo_sb[:], in_=wgo)
         acc_b = {(i, half): bank(2 * i + half) for i, half in groups}
         by_row = [(i, half) for i in range(PACK) for half in range(2)]
-        for a in range(PASSES):
-            for i, half in (by_row if a == PASSES - 1 else groups):
+        order_b = [(a, i, half) for pair in range(2) for a in range(PASSES)
+                   for i in range(2 * pair, 2 * pair + 2) for half in range(2)]
+        for a, i, half in order_b:
+            if True:
                 cols = slice(P * (i % 2), P * (i % 2 + 1))
                 nc.tensor.matmul_mx(
                     out=acc_b[i, half][:],
@@ -187,7 +193,7 @@ def tile_list_bonsai_restraint_scores_kernel(
         z_sc = held("z_sc", [P, M], U8)
         for half in range(2):
             cols = slice(HM * half, HM * (half + 1))
-            x = held("x%d" % half, [P, PACK, HM], F32)
+            x = held("x", [P, PACK, HM], F32)
             for i in range(PACK):
                 nc.vector.tensor_tensor(x[:, i, :], h[i][:].indirect(idx2[:, 16 * half:16 * (half + 1)]),
                                         wt[:, i, cols], ALU.mult)

@@ -22,7 +22,9 @@ PASSES = K // (P * PACK)
 BANK = 512
 PAGES = 3
 SLOT = 4 * T
-SC_AT = 5 * SLOT // 2 + 1024
+ODD_AT = 0
+EVEN_AT = SLOT + N
+SC_AT = EVEN_AT + 3 * SLOT // 2
 SPLIT_TILES = 2
 
 
@@ -51,15 +53,16 @@ def tile_list_bonsai_restraint_scores_kernel(
         idx3 = keep.tile([P, M // 16], U16, name="idx3")
         tab_sc = staged("tab_sc", [P, T], U8, SC_AT)
         w1_sc_raw = held("w1_sc_raw", [P, PASSES, H], U8)
+        w3_sc_raw = held("w3_sc_raw", [P, N], U8)
         v_sc = [held("v_sc%d" % a, [P, S], U8) for a in range(PASSES)]
 
         nc.vector.memset(tab_sc[:].bitcast(I32), 0)
         nc.vector.memset(w1_sc_raw[:].rearrange("p a c -> p (a c)").bitcast(I32), 0)
-        for plane in v_sc:
+        for plane in [w3_sc_raw] + v_sc:
             nc.vector.memset(plane[:].bitcast(I32), 0)
 
         def load_table(a):
-            words = staged("tab%d" % a, [P, T], U32, a % 2 * SLOT)
+            words = staged("tab%d" % a, [P, T], U32, ODD_AT if a % 2 else EVEN_AT)
             nc.sync.dma_start(out=words[:].bitcast(I32),
                               in_=tab_words[a].rearrange("p t i -> p (t i)").bitcast(I32))
             return words
@@ -73,36 +76,37 @@ def tile_list_bonsai_restraint_scores_kernel(
         taste_sb = held("taste_sb", [P, PACK], F32)
         nc.gpsimd.dma_start(out=gain_sb[:], in_=gain.rearrange("(p i) -> p i", i=PACK))
         nc.gpsimd.dma_start(out=taste_sb[:], in_=taste.rearrange("(p i) -> p i", i=PACK))
-        w1_raw = staged("w1_raw", [P, PASSES, 2 * H], U8, SLOT - PASSES * H)
+        w1_raw = staged("w1_raw", [P, PASSES, 2 * H], U8, ODD_AT)
         nc.sync.dma_start(out=w1_raw[:].bitcast(I32), in_=w1_words.rearrange("a p c -> p a c").bitcast(I32))
         nc.sync.dma_start(idx[:], offs)
-        w2_raw = [load_w2(0, 2 * SLOT)]
         nc.sync.dma_start(idx2[:], offs2)
         nc.sync.dma_start(idx3[:], offs3)
-        wgt_sb = held("wgt_sb", [P, M], F32)
-        nc.sync.dma_start(out=wgt_sb[:], in_=wgt)
-        nc.sync.dma_start(out=tab_sc[0:P:4, :].bitcast(I32),
-                          in_=tab_scales[0:2].rearrange("a q t -> (a q) t").bitcast(I32))
-        nc.sync.dma_start(out=tab_sc[2:P:8, :].bitcast(I32), in_=tab_scales[2].bitcast(I32))
+        tab = [load_table(0)]
+        nc.scalar.dma_start(out=tab_sc[0:P:4, :].bitcast(I32),
+                            in_=tab_scales[0:2].rearrange("a q t -> (a q) t").bitcast(I32))
+        nc.scalar.dma_start(out=tab_sc[2:P:8, :].bitcast(I32), in_=tab_scales[2].bitcast(I32))
         for q in range(4):
             nc.scalar.dma_start(out=w1_sc_raw[32 * q:32 * q + 4].bitcast(I32),
                                 in_=w1_scales[:, 4 * q:4 * q + 4, :].rearrange("a r c -> r a c").bitcast(I32))
+        for q in range(4):
+            nc.gpsimd.dma_start(out=w3_sc_raw[32 * q:32 * q + 4, :].bitcast(I32),
+                                in_=w3_scales[0, 4 * q:4 * q + 4, :].bitcast(I32))
 
         w1_q = held("w1_q", [P, PASSES, 2 * H], U8)
         nc.vector.tensor_copy(out=w1_q[:].bitcast(U16).rearrange("p a (i m) -> p a m i", i=PACK),
                               in_=w1_raw[:].bitcast(U16).rearrange("p a (m i) -> p a m i", i=PACK))
-        tab = [load_table(0), load_table(1)]
+        tab.append(load_table(1))
         picked_sc = held("picked_sc", [P, S], U8)
         nc.vector.tensor_copy(picked_sc[:], tab_sc[:].indirect(idx[:]))
-        w1_sc = staged("w1_sc", [P, PASSES, H], U8, SC_AT + 1024)
+        w1_sc = staged("w1_sc", [P, PASSES, H], U8, SC_AT)
         nc.vector.tensor_copy(out=w1_sc[:].rearrange("p a (i m) -> p a m i", i=PACK),
                               in_=w1_sc_raw[:].rearrange("p a (m i) -> p a m i", i=PACK))
         for a in range(PASSES):
             for q in range(4):
                 first, step = (64 * a + 16 * q, 4) if a < 2 else (2 + 32 * q, 8)
-                queue = nc.scalar if a < 2 and q < 3 else nc.gpsimd
+                queue = nc.gpsimd if (a, q) == (1, 3) else nc.scalar
                 queue.dma_start(out=v_sc[a][32 * q:32 * q + 4, :].bitcast(I32),
-                                    in_=picked_sc[first:first + 3 * step + 1:step, :].bitcast(I32))
+                                in_=picked_sc[first:first + 3 * step + 1:step, :].bitcast(I32))
         v = {}
         for a in range(PASSES):
             for half in range(2):
@@ -111,22 +115,23 @@ def tile_list_bonsai_restraint_scores_kernel(
             if a == 0:
                 tab.append(load_table(2))
 
-        w2_raw.extend([load_w2(1, SLOT), load_w2(2, 3 * SLOT // 2)])
-        w3_sc_raw = staged("w3_sc_raw", [P, N], U8, 4 * M)
-        nc.vector.memset(w3_sc_raw[:].bitcast(I32), 0)
-        w3_raw = staged("w3_raw", [P, N], U32, 4 * M + N)
+        w3_sc = staged("w3_sc", [P, N], U8, ODD_AT)
+        nc.vector.tensor_copy(out=w3_sc[:].rearrange("p (b i m) -> p b m i", b=2, i=PACK),
+                              in_=w3_sc_raw[:].rearrange("p (b m i) -> p b m i", b=2, i=PACK))
+        w2_raw = [load_w2(0, ODD_AT + N), load_w2(1, ODD_AT + N + SLOT // 2), load_w2(2, EVEN_AT)]
+        wgt_sb = staged("wgt_sb", [P, M], F32, EVEN_AT + SLOT // 2)
+        nc.sync.dma_start(out=wgt_sb[:], in_=wgt)
+        w3_raw = staged("w3_raw", [P, N], U32, EVEN_AT + SLOT // 2 + 4 * M)
         nc.sync.dma_start(out=w3_raw[:].bitcast(I32), in_=w3_words[0].rearrange("p c i -> p (c i)").bitcast(I32))
-        season_sb = staged("season_sb", [P, PACK, M], F32, 4 * M + 5 * N)
+        season_sb = staged("season_sb", [P, PACK, M], F32, EVEN_AT + SLOT // 2 + 4 * M + 4 * N)
         nc.sync.dma_start(out=season_sb[:], in_=season.rearrange("(p i) m -> p i m", i=PACK))
-        for q in range(4):
-            nc.sync.dma_start(out=w3_sc_raw[32 * q:32 * q + 4, :].bitcast(I32),
-                              in_=w3_scales[0, 4 * q:4 * q + 4, :].bitcast(I32))
 
         groups = [(i, half) for half in range(2) for i in range(PACK)]
         acc_a = {(i, half): bank(2 * i + half) for i, half in groups}
         g = {}
+        by_row = [(i, half) for i in range(PACK) for half in range(2)]
         for a in range(PASSES):
-            for i, half in groups:
+            for i, half in (by_row if a == PASSES - 1 else groups):
                 nc.tensor.matmul_mx(
                     out=acc_a[i, half][:],
                     lhsT=w1_q[:, a, 256 * i:256 * (i + 1)].bitcast(FP4X4),
@@ -134,7 +139,7 @@ def tile_list_bonsai_restraint_scores_kernel(
                     rhs=v[a, half][:].bitcast(FP8X4),
                     rhs_scale=v_sc[a][:, BANK * half:BANK * (half + 1)],
                     start=(a == 0), stop=(a == PASSES - 1))
-        for i, half in groups:
+        for i, half in by_row:
             g[i, half] = held("g%d_%d" % (i, half), [P, BANK], F32)
             nc.scalar.activation(out=g[i, half][:], in_=acc_a[i, half][:], func=ACT.Gelu_apprx_tanh)
 
@@ -142,7 +147,7 @@ def tile_list_bonsai_restraint_scores_kernel(
         w2_sc = {}
         for a in range(PASSES):
             for pair in range(2):
-                rounded = staged("rounded%d" % pair, [P, 2 * P * PACK], BF16, SC_AT - 1024 + pair * 3584)
+                rounded = held("rounded%d" % pair, [P, 2 * P * PACK], BF16)
                 src = w2_raw[a][:].rearrange("p j (m i) -> p m i j", i=PACK)[:, :, 2 * pair:2 * pair + 2, :]
                 dst = rounded[:].rearrange("p (i m j) -> p m i j", i=2, j=PACK)
                 if a == PASSES - 1 and pair == 1:
@@ -153,10 +158,9 @@ def tile_list_bonsai_restraint_scores_kernel(
                 w2_sc[a, pair] = held("w2_sc%d_%d" % (a, pair), [P, 2 * P], U8)
                 nc.vector.quantize_mx(out=w2_q[a, pair][:].bitcast(FP8X4), scales=w2_sc[a, pair][:], in_=rounded[:])
 
-        wgo_sb = staged("wgo_sb", [P, M], F32, SLOT)
+        wgo_sb = staged("wgo_sb", [P, M], F32, ODD_AT + N + SLOT // 2)
         nc.sync.dma_start(out=wgo_sb[:], in_=wgo)
         acc_b = {(i, half): bank(2 * i + half) for i, half in groups}
-        by_row = [(i, half) for i in range(PACK) for half in range(2)]
         order_b = [(a, i, half) for pair in range(2) for a in range(PASSES)
                    for i in range(2 * pair, 2 * pair + 2) for half in range(2)]
         for a, i, half in order_b:
@@ -183,10 +187,6 @@ def tile_list_bonsai_restraint_scores_kernel(
         w3_q = held("w3_q", [P, N], U32)
         nc.scalar.copy(out=w3_q[:].rearrange("p (b i m) -> p b m i", b=2, i=PACK),
                        in_=w3_raw[:].rearrange("p (b m i) -> p b m i", b=2, i=PACK))
-
-        w3_sc = held("w3_sc", [P, N], U8)
-        nc.vector.tensor_copy(out=w3_sc[:].rearrange("p (b i m) -> p b m i", b=2, i=PACK),
-                              in_=w3_sc_raw[:].rearrange("p (b m i) -> p b m i", b=2, i=PACK))
 
         HM = M // 2
         z_q = held("z_q", [P, M], U32)

@@ -19,13 +19,25 @@ FLOPS = 2 * (2 * K * H * S + H * N * M)
 P = 128
 PACK = 4
 PASSES = K // (P * PACK)
+QUADS = 4
 BANK = 512
+BANKS = 8
+HM = M // 2
 PAGES = 3
-SLOT = 4 * T
-ODD_AT = 0
-EVEN_AT = SLOT + N
-SC_AT = EVEN_AT + 3 * SLOT // 2
+Y_BUFS = 4
 SPLIT_TILES = 2
+
+KIB = 1024
+SLOT = 4 * T
+TAB1_AT = 7 * KIB
+W2_LAST_AT = 0
+W3_SC_AT = 8 * KIB
+WGT_AT = 9 * KIB
+W2_FIRST_AT = 11 * KIB
+W2_SECOND_AT = 19 * KIB
+TAB0_AT = 27 * KIB
+TAB2_AT = TAB0_AT + PASSES * H
+TAB_SC_AT = TAB2_AT + SLOT
 
 
 def tile_list_bonsai_restraint_scores_kernel(
@@ -36,7 +48,7 @@ def tile_list_bonsai_restraint_scores_kernel(
     with ExitStack() as ctx:
         keep = ctx.enter_context(tc.tile_pool(name="keep", bufs=1))
         arena = ctx.enter_context(tc.tile_pool(name="arena", bufs=1))
-        ring = ctx.enter_context(tc.tile_pool(name="ring", bufs=4))
+        ring = ctx.enter_context(tc.tile_pool(name="ring", bufs=Y_BUFS))
         psum = ctx.enter_context(tc.psum_pool(name="psum", bufs=1))
 
         def held(name, shape, dtype):
@@ -51,7 +63,7 @@ def tile_list_bonsai_restraint_scores_kernel(
         idx = keep.tile([P, S // 16], U16, name="idx")
         idx2 = keep.tile([P, M // 16], U16, name="idx2")
         idx3 = keep.tile([P, M // 16], U16, name="idx3")
-        tab_sc = staged("tab_sc", [P, T], U8, SC_AT)
+        tab_sc = staged("tab_sc", [P, T], U8, TAB_SC_AT)
         w1_sc_raw = held("w1_sc_raw", [P, PASSES, H], U8)
         w3_sc_raw = held("w3_sc_raw", [P, N], U8)
         v_sc = [held("v_sc%d" % a, [P, S], U8) for a in range(PASSES)]
@@ -62,7 +74,7 @@ def tile_list_bonsai_restraint_scores_kernel(
             nc.vector.memset(plane[:].bitcast(I32), 0)
 
         def load_table(a):
-            words = staged("tab%d" % a, [P, T], U32, ODD_AT if a % 2 else EVEN_AT)
+            words = staged("tab%d" % a, [P, T], U32, [TAB0_AT, TAB1_AT, TAB2_AT][a])
             nc.sync.dma_start(out=words[:].bitcast(I32),
                               in_=tab_words[a].rearrange("p t i -> p (t i)").bitcast(I32))
             return words
@@ -76,7 +88,7 @@ def tile_list_bonsai_restraint_scores_kernel(
         taste_sb = held("taste_sb", [P, PACK], F32)
         nc.gpsimd.dma_start(out=gain_sb[:], in_=gain.rearrange("(p i) -> p i", i=PACK))
         nc.gpsimd.dma_start(out=taste_sb[:], in_=taste.rearrange("(p i) -> p i", i=PACK))
-        w1_raw = staged("w1_raw", [P, PASSES, 2 * H], U8, ODD_AT)
+        w1_raw = staged("w1_raw", [P, PASSES, 2 * H], U8, TAB1_AT)
         nc.sync.dma_start(out=w1_raw[:].bitcast(I32), in_=w1_words.rearrange("a p c -> p a c").bitcast(I32))
         nc.sync.dma_start(idx[:], offs)
         nc.sync.dma_start(idx2[:], offs2)
@@ -85,10 +97,10 @@ def tile_list_bonsai_restraint_scores_kernel(
         nc.scalar.dma_start(out=tab_sc[0:P:4, :].bitcast(I32),
                             in_=tab_scales[0:2].rearrange("a q t -> (a q) t").bitcast(I32))
         nc.scalar.dma_start(out=tab_sc[2:P:8, :].bitcast(I32), in_=tab_scales[2].bitcast(I32))
-        for q in range(4):
+        for q in range(QUADS):
             nc.scalar.dma_start(out=w1_sc_raw[32 * q:32 * q + 4].bitcast(I32),
                                 in_=w1_scales[:, 4 * q:4 * q + 4, :].rearrange("a r c -> r a c").bitcast(I32))
-        for q in range(4):
+        for q in range(QUADS):
             nc.gpsimd.dma_start(out=w3_sc_raw[32 * q:32 * q + 4, :].bitcast(I32),
                                 in_=w3_scales[0, 4 * q:4 * q + 4, :].bitcast(I32))
 
@@ -96,45 +108,54 @@ def tile_list_bonsai_restraint_scores_kernel(
         nc.vector.tensor_copy(out=w1_q[:].bitcast(U16).rearrange("p a (i m) -> p a m i", i=PACK),
                               in_=w1_raw[:].bitcast(U16).rearrange("p a (m i) -> p a m i", i=PACK))
         tab.append(load_table(1))
+
         picked_sc = held("picked_sc", [P, S], U8)
         nc.vector.tensor_copy(picked_sc[:], tab_sc[:].indirect(idx[:]))
-        w1_sc = staged("w1_sc", [P, PASSES, H], U8, SC_AT)
-        nc.vector.tensor_copy(out=w1_sc[:].rearrange("p a (i m) -> p a m i", i=PACK),
-                              in_=w1_sc_raw[:].rearrange("p a (m i) -> p a m i", i=PACK))
         for a in range(PASSES):
-            for q in range(4):
+            for q in range(QUADS):
                 first, step = (64 * a + 16 * q, 4) if a < 2 else (2 + 32 * q, 8)
-                queue = nc.gpsimd if (a, q) == (1, 3) else nc.scalar
+                queue = nc.gpsimd if (a, q) == (1, QUADS - 1) else nc.scalar
                 queue.dma_start(out=v_sc[a][32 * q:32 * q + 4, :].bitcast(I32),
                                 in_=picked_sc[first:first + 3 * step + 1:step, :].bitcast(I32))
-        v = {}
-        for a in range(PASSES):
-            for half in range(2):
-                v[a, half] = held("v%d_%d" % (a, half), [P, BANK], U32)
-                nc.vector.tensor_copy(v[a, half][:], tab[a][:].indirect(idx[:, 32 * half:32 * (half + 1)]))
-            if a == 0:
-                tab.append(load_table(2))
 
-        w3_sc = staged("w3_sc", [P, N], U8, ODD_AT)
+        v = {}
+
+        def gather_words(a):
+            for half in range(2):
+                if a == 0:
+                    v[a, half] = staged("v0_%d" % half, [P, BANK], U32, TAB_SC_AT + 4 * BANK * half)
+                else:
+                    v[a, half] = held("v%d_%d" % (a, half), [P, BANK], U32)
+                nc.vector.tensor_copy(v[a, half][:], tab[a][:].indirect(idx[:, 32 * half:32 * (half + 1)]))
+
+        gather_words(0)
+        tab.append(load_table(2))
+        w1_sc = staged("w1_sc", [P, PASSES, H], U8, TAB0_AT)
+        nc.vector.tensor_copy(out=w1_sc[:].rearrange("p a (i m) -> p a m i", i=PACK),
+                              in_=w1_sc_raw[:].rearrange("p a (m i) -> p a m i", i=PACK))
+        gather_words(1)
+        gather_words(2)
+
+        w3_sc = staged("w3_sc", [P, N], U8, W3_SC_AT)
         nc.vector.tensor_copy(out=w3_sc[:].rearrange("p (b i m) -> p b m i", b=2, i=PACK),
                               in_=w3_sc_raw[:].rearrange("p (b m i) -> p b m i", b=2, i=PACK))
-        w2_raw = [load_w2(0, ODD_AT + N), load_w2(1, ODD_AT + N + SLOT // 2), load_w2(2, EVEN_AT)]
-        wgt_sb = staged("wgt_sb", [P, M], F32, EVEN_AT + SLOT // 2)
+        w2_raw = [load_w2(0, W2_FIRST_AT), load_w2(1, W2_SECOND_AT), load_w2(2, W2_LAST_AT)]
+        wgt_sb = staged("wgt_sb", [P, M], F32, WGT_AT)
         nc.sync.dma_start(out=wgt_sb[:], in_=wgt)
-        w3_raw = staged("w3_raw", [P, N], U32, EVEN_AT + SLOT // 2 + 4 * M)
+        w3_raw = staged("w3_raw", [P, N], U32, TAB2_AT)
         nc.sync.dma_start(out=w3_raw[:].bitcast(I32), in_=w3_words[0].rearrange("p c i -> p (c i)").bitcast(I32))
-        season_sb = staged("season_sb", [P, PACK, M], F32, EVEN_AT + SLOT // 2 + 4 * M + 4 * N)
+        season_sb = staged("season_sb", [P, PACK, M], F32, TAB2_AT + 4 * N)
         nc.sync.dma_start(out=season_sb[:], in_=season.rearrange("(p i) m -> p i m", i=PACK))
 
-        groups = [(i, half) for half in range(2) for i in range(PACK)]
-        acc_a = {(i, half): bank(2 * i + half) for i, half in groups}
-        g = {}
+        by_half = [(i, half) for half in range(2) for i in range(PACK)]
         by_row = [(i, half) for i in range(PACK) for half in range(2)]
+        acc_a = {(i, half): bank(2 * i + half) for i, half in by_half}
+        g = {}
         for a in range(PASSES):
-            for i, half in (by_row if a == PASSES - 1 else groups):
+            for i, half in (by_row if a == PASSES - 1 else by_half):
                 nc.tensor.matmul_mx(
                     out=acc_a[i, half][:],
-                    lhsT=w1_q[:, a, 256 * i:256 * (i + 1)].bitcast(FP4X4),
+                    lhsT=w1_q[:, a, 2 * P * i:2 * P * (i + 1)].bitcast(FP4X4),
                     lhsT_scale=w1_sc[:, a, P * i:P * (i + 1)],
                     rhs=v[a, half][:].bitcast(FP8X4),
                     rhs_scale=v_sc[a][:, BANK * half:BANK * (half + 1)],
@@ -158,21 +179,21 @@ def tile_list_bonsai_restraint_scores_kernel(
                 w2_sc[a, pair] = held("w2_sc%d_%d" % (a, pair), [P, 2 * P], U8)
                 nc.vector.quantize_mx(out=w2_q[a, pair][:].bitcast(FP8X4), scales=w2_sc[a, pair][:], in_=rounded[:])
 
-        wgo_sb = staged("wgo_sb", [P, M], F32, ODD_AT + N + SLOT // 2)
+        wgo_sb = staged("wgo_sb", [P, M], F32, W2_SECOND_AT)
         nc.sync.dma_start(out=wgo_sb[:], in_=wgo)
-        acc_b = {(i, half): bank(2 * i + half) for i, half in groups}
-        order_b = [(a, i, half) for pair in range(2) for a in range(PASSES)
-                   for i in range(2 * pair, 2 * pair + 2) for half in range(2)]
-        for a, i, half in order_b:
-            if True:
-                cols = slice(P * (i % 2), P * (i % 2 + 1))
-                nc.tensor.matmul_mx(
-                    out=acc_b[i, half][:],
-                    lhsT=w2_q[a, i // 2][:, cols].bitcast(FP8X4),
-                    lhsT_scale=w2_sc[a, i // 2][:, cols],
-                    rhs=v[a, half][:].bitcast(FP8X4),
-                    rhs_scale=v_sc[a][:, BANK * half:BANK * (half + 1)],
-                    start=(a == 0), stop=(a == PASSES - 1))
+
+        acc_b = {(i, half): bank(2 * i + half) for i, half in by_half}
+        for pair in range(2):
+            for a in range(PASSES):
+                for i, half in by_row[4 * pair:4 * (pair + 1)]:
+                    cols = slice(P * (i % 2), P * (i % 2 + 1))
+                    nc.tensor.matmul_mx(
+                        out=acc_b[i, half][:],
+                        lhsT=w2_q[a, pair][:, cols].bitcast(FP8X4),
+                        lhsT_scale=w2_sc[a, pair][:, cols],
+                        rhs=v[a, half][:].bitcast(FP8X4),
+                        rhs_scale=v_sc[a][:, BANK * half:BANK * (half + 1)],
+                        start=(a == 0), stop=(a == PASSES - 1))
 
         wt = held("wt", [P, PACK, M], F32)
         for i in range(PACK):
@@ -188,7 +209,6 @@ def tile_list_bonsai_restraint_scores_kernel(
         nc.scalar.copy(out=w3_q[:].rearrange("p (b i m) -> p b m i", b=2, i=PACK),
                        in_=w3_raw[:].rearrange("p (b m i) -> p b m i", b=2, i=PACK))
 
-        HM = M // 2
         z_q = held("z_q", [P, M], U32)
         z_sc = held("z_sc", [P, M], U8)
         for half in range(2):
@@ -232,5 +252,5 @@ def tile_list_bonsai_restraint_scores_kernel(
             place(tile_n, HM, HM, SPLIT_TILES + tile_n)
             store(tile_n)
         for tile_n in range(SPLIT_TILES, N // P):
-            place(tile_n, 0, M, (SPLIT_TILES + tile_n) % 8)
+            place(tile_n, 0, M, (SPLIT_TILES + tile_n) % BANKS)
             store(tile_n)

from contextlib import ExitStack

import concourse.mybir as mybir

F32 = mybir.dt.float32
BF16 = mybir.dt.bfloat16
I32 = mybir.dt.int32
U32 = mybir.dt.uint32
U16 = mybir.dt.uint16
U8 = mybir.dt.uint8
FP8X4 = mybir.dt.float8_e4m3fn_x4
FP4X4 = mybir.dt.float4_e2m1fn_x4
ACT = mybir.ActivationFunctionType
ALU = mybir.AluOpType

K, T, S, H, M, T2, N = 1536, 4096, 1024, 512, 512, 1024, 1024
FLOPS = 2 * (2 * K * H * S + H * N * M)

P = 128
PACK = 4
PASSES = K // (P * PACK)
QUADS = 4
BANK = 512
BANKS = 8
HM = M // 2
PAGES = 3
Y_BUFS = 4
SPLIT_TILES = 2

KIB = 1024
SLOT = 4 * T
TAB1_AT = 7 * KIB
W2_LAST_AT = 0
W3_SC_AT = 8 * KIB
WGT_AT = 9 * KIB
W2_FIRST_AT = 11 * KIB
W2_SECOND_AT = 19 * KIB
TAB0_AT = 27 * KIB
TAB2_AT = TAB0_AT + PASSES * H
TAB_SC_AT = TAB2_AT + SLOT


def tile_list_bonsai_restraint_scores_kernel(
    tc, tab_words, tab_scales, offs, w1_words, w1_scales, w2, gain, offs2, wgt, taste, season,
    w3_words, w3_scales, offs3, wgo, out,
):
    nc = tc.nc
    with ExitStack() as ctx:
        keep = ctx.enter_context(tc.tile_pool(name="keep", bufs=1))
        arena = ctx.enter_context(tc.tile_pool(name="arena", bufs=1))
        ring = ctx.enter_context(tc.tile_pool(name="ring", bufs=Y_BUFS))
        psum = ctx.enter_context(tc.psum_pool(name="psum", bufs=1))

        def held(name, shape, dtype):
            return keep.tile(shape, dtype, name=name, align_bytes=64)

        def bank(index):
            return psum.tile([P, BANK], F32, name="bank%d" % index)

        def staged(name, shape, dtype, offset):
            return arena.tile(shape, dtype, name=name, align_bytes=64, offset=offset)

        idx = keep.tile([P, S // 16], U16, name="idx")
        idx2 = keep.tile([P, M // 16], U16, name="idx2")
        idx3 = keep.tile([P, M // 16], U16, name="idx3")
        tab_sc = staged("tab_sc", [P, T], U8, TAB_SC_AT)
        w1_sc_raw = held("w1_sc_raw", [P, PASSES, H], U8)
        w3_sc_raw = held("w3_sc_raw", [P, N], U8)
        v_sc = [held("v_sc%d" % a, [P, S], U8) for a in range(PASSES)]

        nc.vector.memset(tab_sc[:].bitcast(I32), 0)
        nc.vector.memset(w1_sc_raw[:].rearrange("p a c -> p (a c)").bitcast(I32), 0)
        for plane in [w3_sc_raw] + v_sc:
            nc.vector.memset(plane[:].bitcast(I32), 0)

        def load_table(a):
            words = staged("tab%d" % a, [P, T], U32, [TAB0_AT, TAB1_AT, TAB2_AT][a])
            nc.sync.dma_start(out=words[:].bitcast(I32),
                              in_=tab_words[a].rearrange("p t i -> p (t i)").bitcast(I32))
            return words

        def load_w2(a, offset):
            rows = staged("w2_raw%d" % a, [P, PACK, H], F32, offset)
            nc.sync.dma_start(out=rows[:], in_=w2[512 * a:512 * (a + 1), :].rearrange("(p j) c -> p j c", j=PACK))
            return rows

        gain_sb = held("gain_sb", [P, PACK], F32)
        taste_sb = held("taste_sb", [P, PACK], F32)
        nc.gpsimd.dma_start(out=gain_sb[:], in_=gain.rearrange("(p i) -> p i", i=PACK))
        nc.gpsimd.dma_start(out=taste_sb[:], in_=taste.rearrange("(p i) -> p i", i=PACK))
        w1_raw = staged("w1_raw", [P, PASSES, 2 * H], U8, TAB1_AT)
        nc.sync.dma_start(out=w1_raw[:].bitcast(I32), in_=w1_words.rearrange("a p c -> p a c").bitcast(I32))
        nc.sync.dma_start(idx[:], offs)
        nc.sync.dma_start(idx2[:], offs2)
        nc.sync.dma_start(idx3[:], offs3)
        tab = [load_table(0)]
        nc.scalar.dma_start(out=tab_sc[0:P:4, :].bitcast(I32),
                            in_=tab_scales[0:2].rearrange("a q t -> (a q) t").bitcast(I32))
        nc.scalar.dma_start(out=tab_sc[2:P:8, :].bitcast(I32), in_=tab_scales[2].bitcast(I32))
        for q in range(QUADS):
            nc.scalar.dma_start(out=w1_sc_raw[32 * q:32 * q + 4].bitcast(I32),
                                in_=w1_scales[:, 4 * q:4 * q + 4, :].rearrange("a r c -> r a c").bitcast(I32))
        for q in range(QUADS):
            nc.gpsimd.dma_start(out=w3_sc_raw[32 * q:32 * q + 4, :].bitcast(I32),
                                in_=w3_scales[0, 4 * q:4 * q + 4, :].bitcast(I32))

        w1_q = held("w1_q", [P, PASSES, 2 * H], U8)
        nc.vector.tensor_copy(out=w1_q[:].bitcast(U16).rearrange("p a (i m) -> p a m i", i=PACK),
                              in_=w1_raw[:].bitcast(U16).rearrange("p a (m i) -> p a m i", i=PACK))
        tab.append(load_table(1))

        picked_sc = held("picked_sc", [P, S], U8)
        nc.vector.tensor_copy(picked_sc[:], tab_sc[:].indirect(idx[:]))
        for a in range(PASSES):
            for q in range(QUADS):
                first, step = (64 * a + 16 * q, 4) if a < 2 else (2 + 32 * q, 8)
                queue = nc.gpsimd if (a, q) == (1, QUADS - 1) else nc.scalar
                queue.dma_start(out=v_sc[a][32 * q:32 * q + 4, :].bitcast(I32),
                                in_=picked_sc[first:first + 3 * step + 1:step, :].bitcast(I32))

        v = {}

        def gather_words(a):
            for half in range(2):
                if a == 0:
                    v[a, half] = staged("v0_%d" % half, [P, BANK], U32, TAB_SC_AT + 4 * BANK * half)
                else:
                    v[a, half] = held("v%d_%d" % (a, half), [P, BANK], U32)
                nc.vector.tensor_copy(v[a, half][:], tab[a][:].indirect(idx[:, 32 * half:32 * (half + 1)]))

        gather_words(0)
        tab.append(load_table(2))
        w1_sc = staged("w1_sc", [P, PASSES, H], U8, TAB0_AT)
        nc.vector.tensor_copy(out=w1_sc[:].rearrange("p a (i m) -> p a m i", i=PACK),
                              in_=w1_sc_raw[:].rearrange("p a (m i) -> p a m i", i=PACK))
        gather_words(1)
        gather_words(2)

        w3_sc = staged("w3_sc", [P, N], U8, W3_SC_AT)
        nc.vector.tensor_copy(out=w3_sc[:].rearrange("p (b i m) -> p b m i", b=2, i=PACK),
                              in_=w3_sc_raw[:].rearrange("p (b m i) -> p b m i", b=2, i=PACK))
        w2_raw = [load_w2(0, W2_FIRST_AT), load_w2(1, W2_SECOND_AT), load_w2(2, W2_LAST_AT)]
        wgt_sb = staged("wgt_sb", [P, M], F32, WGT_AT)
        nc.sync.dma_start(out=wgt_sb[:], in_=wgt)
        w3_raw = staged("w3_raw", [P, N], U32, TAB2_AT)
        nc.sync.dma_start(out=w3_raw[:].bitcast(I32), in_=w3_words[0].rearrange("p c i -> p (c i)").bitcast(I32))
        season_sb = staged("season_sb", [P, PACK, M], F32, TAB2_AT + 4 * N)
        nc.sync.dma_start(out=season_sb[:], in_=season.rearrange("(p i) m -> p i m", i=PACK))

        by_half = [(i, half) for half in range(2) for i in range(PACK)]
        by_row = [(i, half) for i in range(PACK) for half in range(2)]
        acc_a = {(i, half): bank(2 * i + half) for i, half in by_half}
        g = {}
        for a in range(PASSES):
            for i, half in (by_row if a == PASSES - 1 else by_half):
                nc.tensor.matmul_mx(
                    out=acc_a[i, half][:],
                    lhsT=w1_q[:, a, 2 * P * i:2 * P * (i + 1)].bitcast(FP4X4),
                    lhsT_scale=w1_sc[:, a, P * i:P * (i + 1)],
                    rhs=v[a, half][:].bitcast(FP8X4),
                    rhs_scale=v_sc[a][:, BANK * half:BANK * (half + 1)],
                    start=(a == 0), stop=(a == PASSES - 1))
        for i, half in by_row:
            g[i, half] = held("g%d_%d" % (i, half), [P, BANK], F32)
            nc.scalar.activation(out=g[i, half][:], in_=acc_a[i, half][:], func=ACT.Gelu_apprx_tanh)

        w2_q = {}
        w2_sc = {}
        for a in range(PASSES):
            for pair in range(2):
                rounded = held("rounded%d" % pair, [P, 2 * P * PACK], BF16)
                src = w2_raw[a][:].rearrange("p j (m i) -> p m i j", i=PACK)[:, :, 2 * pair:2 * pair + 2, :]
                dst = rounded[:].rearrange("p (i m j) -> p m i j", i=2, j=PACK)
                if a == PASSES - 1 and pair == 1:
                    nc.scalar.copy(out=dst, in_=src)
                else:
                    nc.vector.tensor_copy(out=dst, in_=src)
                w2_q[a, pair] = held("w2_q%d_%d" % (a, pair), [P, 2 * P], U32)
                w2_sc[a, pair] = held("w2_sc%d_%d" % (a, pair), [P, 2 * P], U8)
                nc.vector.quantize_mx(out=w2_q[a, pair][:].bitcast(FP8X4), scales=w2_sc[a, pair][:], in_=rounded[:])

        wgo_sb = staged("wgo_sb", [P, M], F32, W2_SECOND_AT)
        nc.sync.dma_start(out=wgo_sb[:], in_=wgo)

        acc_b = {(i, half): bank(2 * i + half) for i, half in by_half}
        for pair in range(2):
            for a in range(PASSES):
                for i, half in by_row[4 * pair:4 * (pair + 1)]:
                    cols = slice(P * (i % 2), P * (i % 2 + 1))
                    nc.tensor.matmul_mx(
                        out=acc_b[i, half][:],
                        lhsT=w2_q[a, pair][:, cols].bitcast(FP8X4),
                        lhsT_scale=w2_sc[a, pair][:, cols],
                        rhs=v[a, half][:].bitcast(FP8X4),
                        rhs_scale=v_sc[a][:, BANK * half:BANK * (half + 1)],
                        start=(a == 0), stop=(a == PASSES - 1))

        wt = held("wt", [P, PACK, M], F32)
        for i in range(PACK):
            nc.scalar.activation(out=wt[:, i, :], in_=wgt_sb[:], func=ACT.Copy, scale=taste_sb[:, i:i + 1])

        h = [held("h%d" % i, [P, S], F32) for i in range(PACK)]
        for i, half in by_row:
            nc.vector.tensor_tensor(out=g[i, half][:], in0=acc_b[i, half][:], in1=g[i, half][:], op=ALU.min)
            nc.scalar.activation(out=h[i][:, BANK * half:BANK * (half + 1)], in_=g[i, half][:], func=ACT.Copy,
                                 scale=gain_sb[:, i:i + 1])

        w3_q = held("w3_q", [P, N], U32)
        nc.scalar.copy(out=w3_q[:].rearrange("p (b i m) -> p b m i", b=2, i=PACK),
                       in_=w3_raw[:].rearrange("p (b m i) -> p b m i", b=2, i=PACK))

        z_q = held("z_q", [P, M], U32)
        z_sc = held("z_sc", [P, M], U8)
        for half in range(2):
            cols = slice(HM * half, HM * (half + 1))
            x = held("x", [P, PACK, HM], F32)
            for i in range(PACK):
                nc.vector.tensor_tensor(x[:, i, :], h[i][:].indirect(idx2[:, 16 * half:16 * (half + 1)]),
                                        wt[:, i, cols], ALU.mult)
            z = held("z%d" % half, [P, HM * PACK], BF16)
            nc.vector.tensor_tensor(out=z[:].rearrange("p (c u i) -> p c i u", u=4, i=PACK),
                                    in0=x[:].rearrange("p i (c u) -> p c i u", u=4),
                                    in1=season_sb[:, :, cols].rearrange("p i (c u) -> p c i u", u=4), op=ALU.add)
            nc.vector.quantize_mx(out=z_q[:, cols].bitcast(FP8X4), scales=z_sc[:, cols], in_=z[:])

        pages = [held("page%d" % b, [P, T2], F32) for b in range(PAGES)]
        for page in pages:
            nc.vector.memset(page[:], 0.0)
        out_rows = out.rearrange("(b p i) c -> b i p c", b=2, i=PACK)

        def place(tile_n, first, count, bank_index):
            cols = slice(first, first + count)
            acc = bank(bank_index)
            nc.tensor.matmul_mx(
                out=acc[:, 0:count],
                lhsT=w3_q[:, P * tile_n:P * (tile_n + 1)].bitcast(FP8X4),
                lhsT_scale=w3_sc[:, P * tile_n:P * (tile_n + 1)],
                rhs=z_q[:, cols].bitcast(FP8X4), rhs_scale=z_sc[:, cols], start=True, stop=True)
            y = ring.tile([P, M], F32, name="y")
            nc.scalar.activation(out=y[:, 0:count], in_=acc[:, 0:count], func=ACT.Square)
            nc.scalar.activation(out=y[:, 0:count], in_=y[:, 0:count], func=ACT.Abs_reciprocal_sqrt, bias=1.0)
            nc.scalar.activation(out=y[:, 0:count], in_=y[:, 0:count], func=ACT.Square)
            nc.vector.tensor_tensor(pages[tile_n % PAGES][:].indirect(idx3[:, first // 16:(first + count) // 16]),
                                    y[:, 0:count], wgo_sb[:, cols], ALU.mult)

        def store(tile_n):
            nc.sync.dma_start(out=out_rows[tile_n // PACK, tile_n % PACK], in_=pages[tile_n % PAGES][:])

        for tile_n in range(SPLIT_TILES):
            place(tile_n, 0, HM, tile_n)
        for tile_n in range(SPLIT_TILES):
            place(tile_n, HM, HM, SPLIT_TILES + tile_n)
            store(tile_n)
        for tile_n in range(SPLIT_TILES, N // P):
            place(tile_n, 0, M, (SPLIT_TILES + tile_n) % BANKS)
            store(tile_n)
